import numpy as np
import ml_dtypes


def mxq(x, axis, fmt="e4m3"):
    dtype, down = {"e4m3": (ml_dtypes.float8_e4m3fn, 7), "e5m2": (ml_dtypes.float8_e5m2, 14)}[fmt]
    v = np.moveaxis(np.asarray(x, np.float32).astype(ml_dtypes.bfloat16).astype(np.float64), axis, -1)
    blocks = v.reshape(v.shape[:-1] + (-1, 32))
    amax = np.abs(blocks).max(-1, keepdims=True)
    byte = np.maximum(np.where(amax > 0, np.frexp(amax)[1] - 1 + 127, 0) - down, 1)
    scale = np.exp2(byte - 127.0)
    codes = (blocks / scale).astype(np.float32).astype(dtype).astype(np.float64)
    return np.moveaxis((codes * scale).reshape(v.shape), -1, axis)


WIDE = False


def mx_kscale(k):
    if not WIDE:
        return np.ones(k)
    levels = np.array([10, -10, 5, -5, 0])
    if k % 512:
        return np.exp2(np.random.permutation(np.resize(levels, k // 32))).repeat(32)
    a = np.empty((k // 512, 16))
    for p in range(k // 512):
        a[p, :8] = np.random.permutation(np.resize(levels, 8))
        for g in range(8):
            far = levels[np.abs(levels - a[p, g]) >= 10]
            a[p, g + 8] = far[np.random.randint(len(far))]
    return np.exp2(a.ravel()).repeat(32)


def f64(x):
    return np.asarray(x).astype(np.float64)


def striped(idx):
    return np.tile(idx.reshape(-1, 16).T, (8, 1)).astype(np.uint16)


def unstriped(offs):
    return offs[:16].T.reshape(-1).astype(np.int64)


def striped8(idx):
    return np.concatenate([x.reshape(-1, 16).T for x in idx]).astype(np.uint16)


def runs(offs, k):
    lists = np.stack([offs[16 * r : 16 * r + 16].T.reshape(-1) for r in range(8)]).astype(np.int64)
    return lists[np.arange(k) % 512 // 64]


def pack_weight(w):
    k, n = w.shape
    w = f64(np.asarray(w, np.float32).astype(ml_dtypes.bfloat16)).reshape(k // 32, 32, n)
    amax = np.abs(w).max(1)
    byte = np.clip(np.where(amax > 0, np.frexp(amax)[1] - 1 + 127 - 7, 1), 1, 254)
    scaled = (w * np.exp2(127.0 - byte)[:, None, :]).reshape(k, n).astype(np.float32)
    words = np.ascontiguousarray(scaled.reshape(k // 512, 128, 4, n).transpose(0, 1, 3, 2)).astype(ml_dtypes.float8_e4m3fn).view(np.uint8)
    return words, np.ascontiguousarray(byte.astype(np.uint8).reshape(k // 512, 16, n))


def unpack_weight(words, scales):
    g, p, n, _ = words.shape
    vals = np.ascontiguousarray(words).view(ml_dtypes.float8_e4m3fn).astype(np.float64) * np.repeat(np.exp2(scales.astype(np.float64) - 127.0), 8, axis=1)[..., None]
    return vals.transpose(0, 1, 3, 2).reshape(g * 512, n)


K, T, S, H, G, W = 512, 1024, 256, 512, 2048, 192


def setup_inputs():
    n = np.random.standard_normal
    s = mx_kscale(K)[:, None]
    packed_xT = pack_weight(n((K, T)) * s)
    packed_dT = pack_weight(n((K, G)) / s)
    return {
        "x_words": packed_xT[0],
        "x_scales": packed_xT[1],
        "w1": (n((K, H)) / np.sqrt(K) / s).astype(np.float32),
        "w2": (n((K, H)) / np.sqrt(K) / s).astype(np.float32),
        "gs": (np.random.uniform(0.5, 1.5, (K, 1)) * s).astype(np.float32),
        "d_words": packed_dT[0],
        "d_scales": packed_dT[1],
        "offs": striped(np.random.permutation(T)[:S]),
        "two": striped(np.random.permutation(T)[:S]),
        "n1": striped(np.random.permutation(S)),
        "n2": striped(np.random.permutation(S)),
        "k1": striped8(np.random.randint(0, G, (8, H))),
        "n3": striped(np.random.permutation(S)[:W]),
        "n4": striped(np.random.permutation(S)[:W]),
    }


def reference(x_words, x_scales, w1, w2, gs, d_words, d_scales, offs, two, n1, n2, k1, n3, n4):
    d_k1 = unpack_weight(d_words, d_scales)[np.arange(K)[:, None], runs(k1, K)]
    xq = unpack_weight(x_words, x_scales)[:, unstriped(offs)]
    y = mxq(f64(w1), 0, "e4m3").T @ xq
    x_two = unpack_weight(x_words, x_scales)[:, unstriped(two)]
    d = mxq(f64(w2), 0, "e4m3").T @ x_two
    z = f64(gs) * (y * (np.tanh(d[:, unstriped(n1)] - d[:, unstriped(n2)])))
    h = 0.0625 * ((d_k1.T @ mxq(z, 0, "e4m3")))
    old = h[:, unstriped(n3)]
    pa = h[:, unstriped(n4)]
    ra = old - (0.5 * pa)
    out = h.copy()
    out[:, unstriped(n3)] = ra
    return out

@@ -1,0 +1,173 @@
+from contextlib import ExitStack
+
+import concourse.mybir as mybir
+
+K, T, S, H, G, W = 512, 1024, 256, 512, 2048, 192
+FLOPS = 3 * 2 * K * H * S
+
+F32 = mybir.dt.float32
+BF16 = mybir.dt.bfloat16
+I32 = mybir.dt.int32
+U32 = mybir.dt.uint32
+U16 = mybir.dt.uint16
+U8 = mybir.dt.uint8
+FP8X4 = mybir.dt.float8_e4m3fn_x4
+ACT = mybir.ActivationFunctionType
+ALU = mybir.AluOpType
+
+P = 128
+PACK = 4
+HALF = H // 2
+PIECES = ((0, 128), (128, 128))
+W2_SCALAR_M = 80
+
+
+def deal_views(raw, raw_m0, grouped, m0, m1):
+    src = raw[:, :, PACK * (m0 - raw_m0) : PACK * (m1 - raw_m0)].rearrange("p j (m t) -> p m j t", t=PACK)
+    dst = grouped[:, :, m0:m1, :].rearrange("p t m j -> p m j t")
+    return dst, src
+
+
+def tile_picked_twqjointbkdif_none_p_kernel(tc, x_words, x_scales, w1, w2, gs, d_words, d_scales, offs, two, n1, n2, k1, n3, n4, out):
+    nc = tc.nc
+    with ExitStack() as ctx:
+        keep = ctx.enter_context(tc.tile_pool(name="keep", bufs=1))
+        psum = ctx.enter_context(tc.psum_pool(name="psum", bufs=1))
+
+        def sb(name, shape, dtype):
+            return keep.tile(shape, dtype, name=name, align_bytes=64)
+
+        def load_list(name, ap):
+            tile = sb(name, list(ap.shape), U16)
+            nc.sync.dma_start(tile[:], ap)
+            return tile
+
+        def load_weight(name, w, c0, c1):
+            tile = sb(name, [P, PACK, c1 - c0], F32)
+            nc.sync.dma_start(tile[:], w.rearrange("(p j) c -> p j c", j=PACK)[:, :, c0:c1])
+            return tile
+
+        def load_words(name, words, cols):
+            tile = sb(name, [P, cols], U32)
+            nc.sync.dma_start(tile[:].bitcast(I32), words[0].rearrange("p n t -> p (n t)").bitcast(I32))
+            return tile
+
+        xs_tab = sb("xs_tab", [P, T], U8)
+        ds_tab = sb("ds_tab", [P, G], U8)
+        ds_plane = sb("ds_plane", [P, H], U8)
+        nc.gpsimd.memset(xs_tab[:].bitcast(I32), 0)
+        nc.vector.memset(ds_tab[:].bitcast(I32), 0)
+        nc.gpsimd.memset(ds_plane[:].bitcast(I32), 0)
+        for q in range(4):
+            nc.scalar.dma_start(xs_tab[32 * q : 32 * q + 4, :].bitcast(I32), x_scales[0, 4 * q : 4 * q + 4, :].bitcast(I32))
+        nc.scalar.dma_start(ds_tab[0:P:8, :].bitcast(I32), d_scales[0].bitcast(I32))
+
+        two_l = load_list("two_l", two)
+        k1_l = load_list("k1_l", k1)
+        w2_raw = load_weight("w2_raw", w2, 0, H)
+        w1_raw_a = load_weight("w1_raw_a", w1, 0, HALF)
+        xw_tab = load_words("xw_tab", x_words, T)
+        n1_l = load_list("n1_l", n1)
+        n2_l = load_list("n2_l", n2)
+        offs_l = load_list("offs_l", offs)
+        w1_raw_b = load_weight("w1_raw_b", w1, HALF, H)
+        dw_tab = load_words("dw_tab", d_words, G)
+        gs_t = sb("gs_t", [P, PACK], F32)
+        nc.sync.dma_start(gs_t[:], gs.rearrange("(p t) o -> p (t o)", t=PACK))
+        n3_l = load_list("n3_l", n3)
+        n4_l = load_list("n4_l", n4)
+
+        def pick(name, table, lst, n, dtype):
+            tile = sb(name, [P, n], dtype)
+            nc.vector.tensor_copy(tile[:], table[:].indirect(lst[:]))
+            return tile
+
+        def quantize_weight(name, grouped, step):
+            codes = sb(name + "_codes", [P, H], U32)
+            scales = sb(name + "_scales", [P, H], U8)
+            for t in range(0, PACK, step):
+                cols = slice(t * P, (t + step) * P)
+                nc.vector.quantize_mx(codes[:, cols].bitcast(FP8X4), scales[:, cols], grouped[:, t : t + step, :, :].rearrange("p t m j -> p (t m j)"))
+            return codes, scales
+
+        def project(bank, codes, scales, t, xw, xs):
+            cols = slice(t * P, (t + 1) * P)
+            nc.tensor.matmul_mx(bank[:, 0:S], lhsT=codes[:, cols].bitcast(FP8X4), lhsT_scale=scales[:, cols],
+                                rhs=xw[:].bitcast(FP8X4), rhs_scale=xs[:], start=True, stop=True)
+
+        xs_two = pick("xs_two", xs_tab, two_l, S, U8)
+        ds_picked = pick("ds_picked", ds_tab, k1_l, H, U8)
+        for r in range(4):
+            nc.sync.dma_start(ds_plane[r:P:32, :].bitcast(I32), ds_picked[8 * r : P : 32, :].bitcast(I32))
+
+        w2_grouped = sb("w2_grouped", [P, PACK, P, PACK], BF16)
+        w1_grouped = sb("w1_grouped", [P, PACK, P, PACK], BF16)
+        nc.scalar.copy(*deal_views(w2_raw, 0, w2_grouped, 0, W2_SCALAR_M))
+        nc.vector.tensor_copy(*deal_views(w2_raw, 0, w2_grouped, W2_SCALAR_M, P))
+        nc.scalar.copy(*deal_views(w1_raw_a, 0, w1_grouped, 0, P // 2))
+        w2_codes, w2_scales = quantize_weight("w2", w2_grouped, 2)
+        xw_two = pick("xw_two", xw_tab, two_l, S, U32)
+
+        d_rows = []
+        for t in range(PACK):
+            bank = psum.tile([P, S], F32, name="d_bank%d" % t, tag="a%d" % t)
+            project(bank, w2_codes, w2_scales, t, xw_two, xs_two)
+            d_t = sb("d%d" % t, [P, S], F32)
+            nc.vector.tensor_copy(d_t[:], bank[:])
+            d_rows.append(d_t)
+
+        th = {}
+        for c, (j0, n) in enumerate(PIECES):
+            lcols = slice(j0 // 16, (j0 + n) // 16)
+            for t in range(PACK):
+                g1 = sb("g1_%d_%d" % (c, t), [P, n], F32)
+                g2 = sb("g2_%d_%d" % (c, t), [P, n], F32)
+                nc.scalar.activation(g1[:], d_rows[t][:].indirect(n1_l[:, lcols]), ACT.Copy)
+                nc.scalar.activation(g2[:], d_rows[t][:].indirect(n2_l[:, lcols]), ACT.Copy)
+                diff = sb("diff_%d_%d" % (c, t), [P, n], F32)
+                nc.vector.tensor_tensor(diff[:], g1[:], g2[:], ALU.subtract)
+                th[c, t] = sb("th_%d_%d" % (c, t), [P, n], F32)
+                nc.scalar.activation(th[c, t][:], diff[:], ACT.Tanh)
+
+        xs_offs = pick("xs_offs", xs_tab, offs_l, S, U8)
+        xw_offs = pick("xw_offs", xw_tab, offs_l, S, U32)
+        nc.vector.tensor_copy(*deal_views(w1_raw_b, P // 2, w1_grouped, P // 2, P))
+        w1_codes, w1_scales = quantize_weight("w1", w1_grouped, 4)
+        y_banks = []
+        for t in range(PACK):
+            bank = psum.tile([P, S], F32, name="y_bank%d" % t, tag="b%d" % t)
+            project(bank, w1_codes, w1_scales, t, xw_offs, xs_offs)
+            y_banks.append(bank)
+        dw_picked = pick("dw_picked", dw_tab, k1_l, H, U32)
+
+        h_banks = [psum.tile([P, S], F32, name="h_bank%d" % m, tag="a%d" % m) for m in range(4)]
+        h_rows = [sb("h%d" % m, [P, S], F32) for m in range(4)]
+        for c, (j0, n) in enumerate(PIECES):
+            cols = slice(j0, j0 + n)
+            z_planes = sb("z_planes%d" % c, [P, PACK, n], F32)
+            for t in range(PACK):
+                nc.vector.scalar_tensor_tensor(z_planes[:, t, :], th[c, t][:], gs_t[:, t : t + 1], y_banks[t][:, cols], ALU.mult, ALU.mult)
+            z_grouped = sb("z_grouped%d" % c, [P, n, PACK], BF16)
+            nc.vector.tensor_copy(z_grouped[:].rearrange("p (a i) t -> p a t i", i=4), z_planes[:].rearrange("p t (a i) -> p a t i", i=4))
+            z_codes = sb("z_codes%d" % c, [P, n], U32)
+            z_scales = sb("z_scales%d" % c, [P, n], U8)
+            nc.vector.quantize_mx(z_codes[:].bitcast(FP8X4), z_scales[:], z_grouped[:].rearrange("p j t -> p (j t)"))
+            for m in range(4):
+                rows = slice(m * P, (m + 1) * P)
+                nc.tensor.matmul_mx(h_banks[m][:, cols], lhsT=dw_picked[:, rows].bitcast(FP8X4), lhsT_scale=ds_plane[:, rows],
+                                    rhs=z_codes[:].bitcast(FP8X4), rhs_scale=z_scales[:], start=True, stop=True)
+            for m in range(4):
+                if c + 1 < len(PIECES):
+                    nc.scalar.activation(h_rows[m][:, cols], h_banks[m][:, cols], ACT.Copy, scale=0.0625)
+                else:
+                    nc.vector.tensor_scalar_mul(h_rows[m][:, cols], h_banks[m][:, cols], 0.0625)
+
+        for m in range(4):
+            old = sb("old%d" % m, [P, W], F32)
+            pa = sb("pa%d" % m, [P, W], F32)
+            nc.scalar.activation(old[:], h_rows[m][:].indirect(n3_l[:]), ACT.Copy)
+            nc.scalar.activation(pa[:], h_rows[m][:].indirect(n4_l[:]), ACT.Copy)
+            ra = sb("ra%d" % m, [P, W], F32)
+            nc.vector.scalar_tensor_tensor(ra[:], pa[:], -0.5, old[:], ALU.mult, ALU.add)
+            nc.scalar.activation(h_rows[m][:].indirect(n3_l[:]), ra[:], ACT.Copy)
+            nc.sync.dma_start(out[m * P : (m + 1) * P, :], h_rows[m][:])

@@ -17,9 +17,11 @@ ALU = mybir.AluOpType
 
 P = 128
 PACK = 4
-HALF = H // 2
-PIECES = ((0, 128), (128, 128))
-W2_SCALAR_M = 80
+W2_FIRST_M = 96
+N = S // 2
+W2_SCALAR_M = 48
+WHOLE = 2
+SPARE = 16
 
 
 def deal_views(raw, raw_m0, grouped, m0, m1):
@@ -34,8 +36,8 @@ def tile_picked_twqjointbkdif_none_p_kernel(tc, x_words, x_scales, w1, w2, gs, d
         keep = ctx.enter_context(tc.tile_pool(name="keep", bufs=1))
         psum = ctx.enter_context(tc.psum_pool(name="psum", bufs=1))
 
-        def sb(name, shape, dtype):
-            return keep.tile(shape, dtype, name=name, align_bytes=64)
+        def sb(name, shape, dtype, tag=None):
+            return keep.tile(shape, dtype, name=name, tag=tag or name, align_bytes=64)
 
         def load_list(name, ap):
             tile = sb(name, list(ap.shape), U16)
@@ -55,112 +57,117 @@ def tile_picked_twqjointbkdif_none_p_kernel(tc, x_words, x_scales, w1, w2, gs, d
         xs_tab = sb("xs_tab", [P, T], U8)
         ds_tab = sb("ds_tab", [P, G], U8)
         ds_plane = sb("ds_plane", [P, H], U8)
-        nc.gpsimd.memset(xs_tab[:].bitcast(I32), 0)
+        nc.vector.memset(xs_tab[:].bitcast(I32), 0)
         nc.vector.memset(ds_tab[:].bitcast(I32), 0)
-        nc.gpsimd.memset(ds_plane[:].bitcast(I32), 0)
-        for q in range(4):
-            nc.scalar.dma_start(xs_tab[32 * q : 32 * q + 4, :].bitcast(I32), x_scales[0, 4 * q : 4 * q + 4, :].bitcast(I32))
-        nc.scalar.dma_start(ds_tab[0:P:8, :].bitcast(I32), d_scales[0].bitcast(I32))
+        nc.vector.memset(ds_plane[:].bitcast(I32), 0)
 
         two_l = load_list("two_l", two)
-        k1_l = load_list("k1_l", k1)
-        w2_raw = load_weight("w2_raw", w2, 0, H)
-        w1_raw_a = load_weight("w1_raw_a", w1, 0, HALF)
+        offs_l = load_list("offs_l", offs)
         xw_tab = load_words("xw_tab", x_words, T)
+        for q in range(4):
+            nc.sync.dma_start(xs_tab[32 * q : 32 * q + 4, :].bitcast(I32), x_scales[0, 4 * q : 4 * q + 4, :].bitcast(I32))
+        w2_raw_a = load_weight("w2_raw_a", w2, 0, PACK * W2_FIRST_M)
+        w2_raw_b = load_weight("w2_raw_b", w2, PACK * W2_FIRST_M, H)
         n1_l = load_list("n1_l", n1)
         n2_l = load_list("n2_l", n2)
-        offs_l = load_list("offs_l", offs)
-        w1_raw_b = load_weight("w1_raw_b", w1, HALF, H)
+        k1_l = load_list("k1_l", k1)
+        nc.sync.dma_start(ds_tab[0:P:8, :].bitcast(I32), d_scales[0].bitcast(I32))
         dw_tab = load_words("dw_tab", d_words, G)
+        w1_raw = load_weight("w1_raw", w1, 0, H)
         gs_t = sb("gs_t", [P, PACK], F32)
         nc.sync.dma_start(gs_t[:], gs.rearrange("(p t) o -> p (t o)", t=PACK))
         n3_l = load_list("n3_l", n3)
         n4_l = load_list("n4_l", n4)
 
-        def pick(name, table, lst, n, dtype):
-            tile = sb(name, [P, n], dtype)
+        def pick(name, table, lst, n, dtype, tag=None):
+            tile = sb(name, [P, n], dtype, tag)
             nc.vector.tensor_copy(tile[:], table[:].indirect(lst[:]))
             return tile
 
-        def quantize_weight(name, grouped, step):
+        def quantize_weight(name, grouped, cuts):
             codes = sb(name + "_codes", [P, H], U32)
             scales = sb(name + "_scales", [P, H], U8)
-            for t in range(0, PACK, step):
-                cols = slice(t * P, (t + step) * P)
-                nc.vector.quantize_mx(codes[:, cols].bitcast(FP8X4), scales[:, cols], grouped[:, t : t + step, :, :].rearrange("p t m j -> p (t m j)"))
+            for t0, t1 in zip(cuts, cuts[1:]):
+                cols = slice(t0 * P, t1 * P)
+                nc.vector.quantize_mx(codes[:, cols].bitcast(FP8X4), scales[:, cols], grouped[:, t0:t1, :, :].rearrange("p t m j -> p (t m j)"))
             return codes, scales
 
         def project(bank, codes, scales, t, xw, xs):
             cols = slice(t * P, (t + 1) * P)
-            nc.tensor.matmul_mx(bank[:, 0:S], lhsT=codes[:, cols].bitcast(FP8X4), lhsT_scale=scales[:, cols],
+            nc.tensor.matmul_mx(bank, lhsT=codes[:, cols].bitcast(FP8X4), lhsT_scale=scales[:, cols],
                                 rhs=xw[:].bitcast(FP8X4), rhs_scale=xs[:], start=True, stop=True)
 
         xs_two = pick("xs_two", xs_tab, two_l, S, U8)
+        xw_two = pick("xw_two", xw_tab, two_l, S, U32)
+        xs_offs = pick("xs_offs", xs_tab, offs_l, S, U8)
+        w2_grouped = sb("w2_grouped", [P, PACK, P, PACK], BF16)
+        w1_grouped = sb("w1_grouped", [P, PACK, P, PACK], BF16)
+        nc.scalar.copy(*deal_views(w2_raw_a, 0, w2_grouped, 0, W2_SCALAR_M))
+        nc.vector.tensor_copy(*deal_views(w2_raw_a, 0, w2_grouped, W2_SCALAR_M, W2_FIRST_M))
+        nc.vector.tensor_copy(*deal_views(w2_raw_b, W2_FIRST_M, w2_grouped, W2_FIRST_M, P))
+        w2_codes, w2_scales = quantize_weight("w2", w2_grouped, (0, 1, 4))
+
+        d_rows = [sb("d%d" % t, [P, S + SPARE if t < WHOLE else S], F32) for t in range(PACK)]
+        for t in range(WHOLE):
+            nc.vector.memset(d_rows[t][:, S : S + SPARE], 0.0)
+        for t in range(PACK):
+            bank = psum.tile([P, S], F32, name="d_bank%d" % t, tag="a%d" % t)
+            project(bank[:], w2_codes, w2_scales, t, xw_two, xs_two)
+            nc.vector.tensor_copy(d_rows[t][:, 0:S], bank[:])
+
+        xw_offs = pick("xw_offs", xw_tab, offs_l, S, U32, tag="xw_two")
         ds_picked = pick("ds_picked", ds_tab, k1_l, H, U8)
         for r in range(4):
             nc.sync.dma_start(ds_plane[r:P:32, :].bitcast(I32), ds_picked[8 * r : P : 32, :].bitcast(I32))
-
-        w2_grouped = sb("w2_grouped", [P, PACK, P, PACK], BF16)
-        w1_grouped = sb("w1_grouped", [P, PACK, P, PACK], BF16)
-        nc.scalar.copy(*deal_views(w2_raw, 0, w2_grouped, 0, W2_SCALAR_M))
-        nc.vector.tensor_copy(*deal_views(w2_raw, 0, w2_grouped, W2_SCALAR_M, P))
-        nc.scalar.copy(*deal_views(w1_raw_a, 0, w1_grouped, 0, P // 2))
-        w2_codes, w2_scales = quantize_weight("w2", w2_grouped, 2)
-        xw_two = pick("xw_two", xw_tab, two_l, S, U32)
-
-        d_rows = []
-        for t in range(PACK):
-            bank = psum.tile([P, S], F32, name="d_bank%d" % t, tag="a%d" % t)
-            project(bank, w2_codes, w2_scales, t, xw_two, xs_two)
-            d_t = sb("d%d" % t, [P, S], F32)
-            nc.vector.tensor_copy(d_t[:], bank[:])
-            d_rows.append(d_t)
-
-        th = {}
-        for c, (j0, n) in enumerate(PIECES):
-            lcols = slice(j0 // 16, (j0 + n) // 16)
-            for t in range(PACK):
-                g1 = sb("g1_%d_%d" % (c, t), [P, n], F32)
-                g2 = sb("g2_%d_%d" % (c, t), [P, n], F32)
-                nc.scalar.activation(g1[:], d_rows[t][:].indirect(n1_l[:, lcols]), ACT.Copy)
-                nc.scalar.activation(g2[:], d_rows[t][:].indirect(n2_l[:, lcols]), ACT.Copy)
-                diff = sb("diff_%d_%d" % (c, t), [P, n], F32)
-                nc.vector.tensor_tensor(diff[:], g1[:], g2[:], ALU.subtract)
-                th[c, t] = sb("th_%d_%d" % (c, t), [P, n], F32)
-                nc.scalar.activation(th[c, t][:], diff[:], ACT.Tanh)
-
-        xs_offs = pick("xs_offs", xs_tab, offs_l, S, U8)
-        xw_offs = pick("xw_offs", xw_tab, offs_l, S, U32)
-        nc.vector.tensor_copy(*deal_views(w1_raw_b, P // 2, w1_grouped, P // 2, P))
-        w1_codes, w1_scales = quantize_weight("w1", w1_grouped, 4)
-        y_banks = []
-        for t in range(PACK):
-            bank = psum.tile([P, S], F32, name="y_bank%d" % t, tag="b%d" % t)
-            project(bank, w1_codes, w1_scales, t, xw_offs, xs_offs)
-            y_banks.append(bank)
         dw_picked = pick("dw_picked", dw_tab, k1_l, H, U32)
+        nc.vector.tensor_copy(*deal_views(w1_raw, 0, w1_grouped, 0, P))
+        w1_codes, w1_scales = quantize_weight("w1", w1_grouped, (0, 4))
+        y_banks = [psum.tile([P, 2, S], F32, name="y_bank%d" % b) for b in range(2)]
+        for t in range(PACK):
+            project(y_banks[t // 2][:, t % 2, :], w1_codes, w1_scales, t, xw_offs, xs_offs)
 
-        h_banks = [psum.tile([P, S], F32, name="h_bank%d" % m, tag="a%d" % m) for m in range(4)]
+        h_first = psum.tile([P, 4, N], F32, name="h_first")
+        h_second = [psum.tile([P, N], F32, name="h_second%d" % m, tag="a%d" % m) for m in range(4)]
+        h_psum = [[h_first[:, m, :] for m in range(4)], [bank[:] for bank in h_second]]
         h_rows = [sb("h%d" % m, [P, S], F32) for m in range(4)]
-        for c, (j0, n) in enumerate(PIECES):
-            cols = slice(j0, j0 + n)
-            z_planes = sb("z_planes%d" % c, [P, PACK, n], F32)
-            for t in range(PACK):
-                nc.vector.scalar_tensor_tensor(z_planes[:, t, :], th[c, t][:], gs_t[:, t : t + 1], y_banks[t][:, cols], ALU.mult, ALU.mult)
-            z_grouped = sb("z_grouped%d" % c, [P, n, PACK], BF16)
-            nc.vector.tensor_copy(z_grouped[:].rearrange("p (a i) t -> p a t i", i=4), z_planes[:].rearrange("p t (a i) -> p a t i", i=4))
-            z_codes = sb("z_codes%d" % c, [P, n], U32)
-            z_scales = sb("z_scales%d" % c, [P, n], U8)
+        z_planes = sb("z_planes", [P, PACK, S], F32)
+
+        def gate(t, j0, n):
+            lcols = slice(j0 // 16, (j0 + n) // 16)
+            g1 = sb("g1_%d_%d" % (t, j0), [P, n], F32)
+            g2 = sb("g2_%d_%d" % (t, j0), [P, n], F32)
+            nc.scalar.activation(g1[:], d_rows[t][:].indirect(n1_l[:, lcols]), ACT.Copy)
+            nc.scalar.activation(g2[:], d_rows[t][:].indirect(n2_l[:, lcols]), ACT.Copy)
+            diff = sb("diff_%d_%d" % (t, j0), [P, n], F32)
+            nc.gpsimd.tensor_tensor(diff[:], g1[:], g2[:], ALU.subtract)
+            th = sb("th_%d_%d" % (t, j0), [P, n], F32)
+            nc.scalar.activation(th[:], diff[:], ACT.Tanh)
+            nc.vector.scalar_tensor_tensor(z_planes[:, t, j0 : j0 + n], th[:], gs_t[:, t : t + 1], y_banks[t // 2][:, t % 2, j0 : j0 + n], ALU.mult, ALU.mult)
+
+        def coded_product(c):
+            cols = slice(c * N, (c + 1) * N)
+            z_grouped = sb("z_grouped%d" % c, [P, N, PACK], BF16)
+            nc.vector.tensor_copy(z_grouped[:].rearrange("p (a i) t -> p a t i", i=4), z_planes[:, :, cols].rearrange("p t (a i) -> p a t i", i=4))
+            z_codes = sb("z_codes%d" % c, [P, N], U32)
+            z_scales = sb("z_scales%d" % c, [P, N], U8)
             nc.vector.quantize_mx(z_codes[:].bitcast(FP8X4), z_scales[:], z_grouped[:].rearrange("p j t -> p (j t)"))
             for m in range(4):
                 rows = slice(m * P, (m + 1) * P)
-                nc.tensor.matmul_mx(h_banks[m][:, cols], lhsT=dw_picked[:, rows].bitcast(FP8X4), lhsT_scale=ds_plane[:, rows],
+                nc.tensor.matmul_mx(h_psum[c][m], lhsT=dw_picked[:, rows].bitcast(FP8X4), lhsT_scale=ds_plane[:, rows],
                                     rhs=z_codes[:].bitcast(FP8X4), rhs_scale=z_scales[:], start=True, stop=True)
-            for m in range(4):
-                if c + 1 < len(PIECES):
-                    nc.scalar.activation(h_rows[m][:, cols], h_banks[m][:, cols], ACT.Copy, scale=0.0625)
-                else:
-                    nc.vector.tensor_scalar_mul(h_rows[m][:, cols], h_banks[m][:, cols], 0.0625)
+
+        for t in range(WHOLE):
+            gate(t, 0, S)
+        for t in range(WHOLE, PACK):
+            gate(t, 0, N)
+        coded_product(0)
+        for t in range(WHOLE, PACK):
+            gate(t, N, N)
+        for m in range(4):
+            nc.scalar.activation(h_rows[m][:, 0:N], h_psum[0][m], ACT.Copy, scale=0.0625)
+        coded_product(1)
+        for m in range(4):
+            nc.vector.tensor_scalar_mul(h_rows[m][:, N:S], h_psum[1][m], 0.0625)
 
         for m in range(4):
             old = sb("old%d" % m, [P, W], F32)

@@ -17,10 +17,8 @@ ALU = mybir.AluOpType
 
 P = 128
 PACK = 4
-W2_FIRST_M = 96
 N = S // 2
-W2_SCALAR_M = 48
-WHOLE = 2
+W2_SCALAR_M = 42
 SPARE = 16
 
 
@@ -62,18 +60,17 @@ def tile_picked_twqjointbkdif_none_p_kernel(tc, x_words, x_scales, w1, w2, gs, d
         nc.vector.memset(ds_plane[:].bitcast(I32), 0)
 
         two_l = load_list("two_l", two)
-        offs_l = load_list("offs_l", offs)
         xw_tab = load_words("xw_tab", x_words, T)
+        offs_l = load_list("offs_l", offs)
         for q in range(4):
             nc.sync.dma_start(xs_tab[32 * q : 32 * q + 4, :].bitcast(I32), x_scales[0, 4 * q : 4 * q + 4, :].bitcast(I32))
-        w2_raw_a = load_weight("w2_raw_a", w2, 0, PACK * W2_FIRST_M)
-        w2_raw_b = load_weight("w2_raw_b", w2, PACK * W2_FIRST_M, H)
+        w2_raw = load_weight("w2_raw", w2, 0, H)
         n1_l = load_list("n1_l", n1)
         n2_l = load_list("n2_l", n2)
         k1_l = load_list("k1_l", k1)
         nc.sync.dma_start(ds_tab[0:P:8, :].bitcast(I32), d_scales[0].bitcast(I32))
-        dw_tab = load_words("dw_tab", d_words, G)
         w1_raw = load_weight("w1_raw", w1, 0, H)
+        dw_tab = load_words("dw_tab", d_words, G)
         gs_t = sb("gs_t", [P, PACK], F32)
         nc.sync.dma_start(gs_t[:], gs.rearrange("(p t) o -> p (t o)", t=PACK))
         n3_l = load_list("n3_l", n3)
@@ -102,72 +99,71 @@ def tile_picked_twqjointbkdif_none_p_kernel(tc, x_words, x_scales, w1, w2, gs, d
         xs_offs = pick("xs_offs", xs_tab, offs_l, S, U8)
         w2_grouped = sb("w2_grouped", [P, PACK, P, PACK], BF16)
         w1_grouped = sb("w1_grouped", [P, PACK, P, PACK], BF16)
-        nc.scalar.copy(*deal_views(w2_raw_a, 0, w2_grouped, 0, W2_SCALAR_M))
-        nc.vector.tensor_copy(*deal_views(w2_raw_a, 0, w2_grouped, W2_SCALAR_M, W2_FIRST_M))
-        nc.vector.tensor_copy(*deal_views(w2_raw_b, W2_FIRST_M, w2_grouped, W2_FIRST_M, P))
+        nc.scalar.copy(*deal_views(w2_raw, 0, w2_grouped, 0, W2_SCALAR_M))
+        nc.vector.tensor_copy(*deal_views(w2_raw, 0, w2_grouped, W2_SCALAR_M, P))
         w2_codes, w2_scales = quantize_weight("w2", w2_grouped, (0, 1, 4))
 
-        d_rows = [sb("d%d" % t, [P, S + SPARE if t < WHOLE else S], F32) for t in range(PACK)]
-        for t in range(WHOLE):
+        d_rows = [sb("d%d" % t, [P, S + SPARE], F32) for t in range(PACK)]
+        for t in range(PACK):
             nc.vector.memset(d_rows[t][:, S : S + SPARE], 0.0)
         for t in range(PACK):
             bank = psum.tile([P, S], F32, name="d_bank%d" % t, tag="a%d" % t)
             project(bank[:], w2_codes, w2_scales, t, xw_two, xs_two)
-            nc.vector.tensor_copy(d_rows[t][:, 0:S], bank[:])
+            if t == 0:
+                nc.vector.tensor_copy(d_rows[t][:, 0:S], bank[:])
+            else:
+                nc.scalar.copy(d_rows[t][:, 0:S], bank[:])
 
-        xw_offs = pick("xw_offs", xw_tab, offs_l, S, U32, tag="xw_two")
         ds_picked = pick("ds_picked", ds_tab, k1_l, H, U8)
         for r in range(4):
             nc.sync.dma_start(ds_plane[r:P:32, :].bitcast(I32), ds_picked[8 * r : P : 32, :].bitcast(I32))
-        dw_picked = pick("dw_picked", dw_tab, k1_l, H, U32)
         nc.vector.tensor_copy(*deal_views(w1_raw, 0, w1_grouped, 0, P))
+        xw_offs = pick("xw_offs", xw_tab, offs_l, S, U32, tag="w1_raw")
         w1_codes, w1_scales = quantize_weight("w1", w1_grouped, (0, 4))
         y_banks = [psum.tile([P, 2, S], F32, name="y_bank%d" % b) for b in range(2)]
         for t in range(PACK):
             project(y_banks[t // 2][:, t % 2, :], w1_codes, w1_scales, t, xw_offs, xs_offs)
+        dw_picked = pick("dw_picked", dw_tab, k1_l, H, U32)
 
-        h_first = psum.tile([P, 4, N], F32, name="h_first")
-        h_second = [psum.tile([P, N], F32, name="h_second%d" % m, tag="a%d" % m) for m in range(4)]
-        h_psum = [[h_first[:, m, :] for m in range(4)], [bank[:] for bank in h_second]]
         h_rows = [sb("h%d" % m, [P, S], F32) for m in range(4)]
         z_planes = sb("z_planes", [P, PACK, S], F32)
 
-        def gate(t, j0, n):
-            lcols = slice(j0 // 16, (j0 + n) // 16)
-            g1 = sb("g1_%d_%d" % (t, j0), [P, n], F32)
-            g2 = sb("g2_%d_%d" % (t, j0), [P, n], F32)
-            nc.scalar.activation(g1[:], d_rows[t][:].indirect(n1_l[:, lcols]), ACT.Copy)
-            nc.scalar.activation(g2[:], d_rows[t][:].indirect(n2_l[:, lcols]), ACT.Copy)
-            diff = sb("diff_%d_%d" % (t, j0), [P, n], F32)
-            nc.gpsimd.tensor_tensor(diff[:], g1[:], g2[:], ALU.subtract)
-            th = sb("th_%d_%d" % (t, j0), [P, n], F32)
-            nc.scalar.activation(th[:], diff[:], ACT.Tanh)
-            nc.vector.scalar_tensor_tensor(z_planes[:, t, j0 : j0 + n], th[:], gs_t[:, t : t + 1], y_banks[t // 2][:, t % 2, j0 : j0 + n], ALU.mult, ALU.mult)
+        diffs = sb("diffs", [P, PACK, S], F32, tag="dw_tab")
+        for t in range(PACK):
+            g1 = sb("g1_%d" % t, [P, S], F32)
+            g2 = sb("g2_%d" % t, [P, S], F32)
+            nc.scalar.activation(g1[:], d_rows[t][:].indirect(n1_l[:]), ACT.Copy)
+            nc.scalar.activation(g2[:], d_rows[t][:].indirect(n2_l[:]), ACT.Copy)
+            nc.vector.tensor_tensor(diffs[:, t, :], g1[:], g2[:], ALU.subtract)
+        for t in range(PACK):
+            th = sb("th_%d" % t, [P, S], F32)
+            nc.scalar.activation(th[:], diffs[:, t, :], ACT.Tanh)
+            nc.vector.scalar_tensor_tensor(z_planes[:, t, :], th[:], gs_t[:, t : t + 1], y_banks[t // 2][:, t % 2, :], ALU.mult, ALU.mult)
 
-        def coded_product(c):
-            cols = slice(c * N, (c + 1) * N)
-            z_grouped = sb("z_grouped%d" % c, [P, N, PACK], BF16)
-            nc.vector.tensor_copy(z_grouped[:].rearrange("p (a i) t -> p a t i", i=4), z_planes[:, :, cols].rearrange("p t (a i) -> p a t i", i=4))
-            z_codes = sb("z_codes%d" % c, [P, N], U32)
-            z_scales = sb("z_scales%d" % c, [P, N], U8)
-            nc.vector.quantize_mx(z_codes[:].bitcast(FP8X4), z_scales[:], z_grouped[:].rearrange("p j t -> p (j t)"))
-            for m in range(4):
-                rows = slice(m * P, (m + 1) * P)
-                nc.tensor.matmul_mx(h_psum[c][m], lhsT=dw_picked[:, rows].bitcast(FP8X4), lhsT_scale=ds_plane[:, rows],
-                                    rhs=z_codes[:].bitcast(FP8X4), rhs_scale=z_scales[:], start=True, stop=True)
+        halves = [slice(c * N, (c + 1) * N) for c in range(2)]
+        z_grouped = [sb("z_grouped%d" % c, [P, N, PACK], BF16) for c in range(2)]
+        z_codes = sb("z_codes", [P, S], U32)
+        z_scales = sb("z_scales", [P, S], U8)
+        for c in range(2):
+            nc.vector.tensor_copy(z_grouped[c][:].rearrange("p (a i) t -> p a t i", i=4), z_planes[:, :, halves[c]].rearrange("p t (a i) -> p a t i", i=4))
+        for c in range(2):
+            nc.vector.quantize_mx(z_codes[:, halves[c]].bitcast(FP8X4), z_scales[:, halves[c]], z_grouped[c][:].rearrange("p j t -> p (j t)"))
 
-        for t in range(WHOLE):
-            gate(t, 0, S)
-        for t in range(WHOLE, PACK):
-            gate(t, 0, N)
-        coded_product(0)
-        for t in range(WHOLE, PACK):
-            gate(t, N, N)
-        for m in range(4):
-            nc.scalar.activation(h_rows[m][:, 0:N], h_psum[0][m], ACT.Copy, scale=0.0625)
-        coded_product(1)
-        for m in range(4):
-            nc.vector.tensor_scalar_mul(h_rows[m][:, N:S], h_psum[1][m], 0.0625)
+        def coded_product(bank, m, cols):
+            rows = slice(m * P, (m + 1) * P)
+            nc.tensor.matmul_mx(bank[:], lhsT=dw_picked[:, rows].bitcast(FP8X4), lhsT_scale=ds_plane[:, rows],
+                                rhs=z_codes[:, cols].bitcast(FP8X4), rhs_scale=z_scales[:, cols], start=True, stop=True)
+
+        h_left = psum.tile([P, N], F32, name="h_left")
+        coded_product(h_left, 0, halves[0])
+        nc.scalar.activation(h_rows[0][:, halves[0]], h_left[:], ACT.Copy, scale=0.0625)
+        h_right = psum.tile([P, N], F32, name="h_right", tag="a0")
+        coded_product(h_right, 0, halves[1])
+        nc.vector.tensor_scalar_mul(h_rows[0][:, halves[1]], h_right[:], 0.0625)
+        for m in range(1, 4):
+            h_bank = psum.tile([P, S], F32, name="h_bank%d" % m, tag="a%d" % m)
+            coded_product(h_bank, m, slice(0, S))
+            nc.vector.tensor_scalar_mul(h_rows[m][:], h_bank[:], 0.0625)
 
         for m in range(4):
             old = sb("old%d" % m, [P, W], F32)

@@ -18,6 +18,7 @@ ALU = mybir.AluOpType
 P = 128
 PACK = 4
 N = S // 2
+W1_SCALAR_M = 48
 W2_SCALAR_M = 42
 SPARE = 16
 
@@ -59,18 +60,21 @@ def tile_picked_twqjointbkdif_none_p_kernel(tc, x_words, x_scales, w1, w2, gs, d
         nc.vector.memset(ds_tab[:].bitcast(I32), 0)
         nc.vector.memset(ds_plane[:].bitcast(I32), 0)
 
-        two_l = load_list("two_l", two)
         xw_tab = load_words("xw_tab", x_words, T)
+        two_l = load_list("two_l", two)
         offs_l = load_list("offs_l", offs)
         for q in range(4):
             nc.sync.dma_start(xs_tab[32 * q : 32 * q + 4, :].bitcast(I32), x_scales[0, 4 * q : 4 * q + 4, :].bitcast(I32))
         w2_raw = load_weight("w2_raw", w2, 0, H)
         n1_l = load_list("n1_l", n1)
         n2_l = load_list("n2_l", n2)
+        w1_raw = sb("w1_raw", [P, PACK, H], F32)
+        w1_rows = w1.rearrange("(p j) c -> p j c", j=PACK)
+        nc.sync.dma_start(w1_raw[:, :, 0 : H // 2], w1_rows[:, :, 0 : H // 2])
         k1_l = load_list("k1_l", k1)
         nc.sync.dma_start(ds_tab[0:P:8, :].bitcast(I32), d_scales[0].bitcast(I32))
-        w1_raw = load_weight("w1_raw", w1, 0, H)
         dw_tab = load_words("dw_tab", d_words, G)
+        nc.sync.dma_start(w1_raw[:, :, H // 2 : H], w1_rows[:, :, H // 2 : H])
         gs_t = sb("gs_t", [P, PACK], F32)
         nc.sync.dma_start(gs_t[:], gs.rearrange("(p t) o -> p (t o)", t=PACK))
         n3_l = load_list("n3_l", n3)
@@ -82,16 +86,18 @@ def tile_picked_twqjointbkdif_none_p_kernel(tc, x_words, x_scales, w1, w2, gs, d
             return tile
 
         def quantize_weight(name, grouped, cuts):
-            codes = sb(name + "_codes", [P, H], U32)
-            scales = sb(name + "_scales", [P, H], U8)
+            tiles = []
             for t0, t1 in zip(cuts, cuts[1:]):
-                cols = slice(t0 * P, t1 * P)
-                nc.vector.quantize_mx(codes[:, cols].bitcast(FP8X4), scales[:, cols], grouped[:, t0:t1, :, :].rearrange("p t m j -> p (t m j)"))
-            return codes, scales
+                codes = sb("%s_codes%d" % (name, t0), [P, (t1 - t0) * P], U32)
+                scales = sb("%s_scales%d" % (name, t0), [P, (t1 - t0) * P], U8)
+                nc.vector.quantize_mx(codes[:].bitcast(FP8X4), scales[:], grouped[:, t0:t1, :, :].rearrange("p t m j -> p (t m j)"))
+                for t in range(t1 - t0):
+                    tiles.append((codes[:, t * P : (t + 1) * P], scales[:, t * P : (t + 1) * P]))
+            return tiles
 
-        def project(bank, codes, scales, t, xw, xs):
-            cols = slice(t * P, (t + 1) * P)
-            nc.tensor.matmul_mx(bank, lhsT=codes[:, cols].bitcast(FP8X4), lhsT_scale=scales[:, cols],
+        def project(bank, weight, xw, xs):
+            codes, scales = weight
+            nc.tensor.matmul_mx(bank, lhsT=codes.bitcast(FP8X4), lhsT_scale=scales,
                                 rhs=xw[:].bitcast(FP8X4), rhs_scale=xs[:], start=True, stop=True)
 
         xs_two = pick("xs_two", xs_tab, two_l, S, U8)
@@ -101,46 +107,49 @@ def tile_picked_twqjointbkdif_none_p_kernel(tc, x_words, x_scales, w1, w2, gs, d
         w1_grouped = sb("w1_grouped", [P, PACK, P, PACK], BF16)
         nc.scalar.copy(*deal_views(w2_raw, 0, w2_grouped, 0, W2_SCALAR_M))
         nc.vector.tensor_copy(*deal_views(w2_raw, 0, w2_grouped, W2_SCALAR_M, P))
-        w2_codes, w2_scales = quantize_weight("w2", w2_grouped, (0, 1, 4))
+        nc.scalar.copy(*deal_views(w1_raw, 0, w1_grouped, 0, W1_SCALAR_M))
+        w2_tiles = quantize_weight("w2", w2_grouped, (0, 1, 4))
+
+        ds_picked = pick("ds_picked", ds_tab, k1_l, H, U8, tag="w2_raw")
+        for r in range(4):
+            nc.sync.dma_start(ds_plane[r:P:32, :].bitcast(I32), ds_picked[8 * r : P : 32, :].bitcast(I32))
 
         d_rows = [sb("d%d" % t, [P, S + SPARE], F32) for t in range(PACK)]
         for t in range(PACK):
             nc.vector.memset(d_rows[t][:, S : S + SPARE], 0.0)
         for t in range(PACK):
             bank = psum.tile([P, S], F32, name="d_bank%d" % t, tag="a%d" % t)
-            project(bank[:], w2_codes, w2_scales, t, xw_two, xs_two)
-            if t == 0:
+            project(bank[:], w2_tiles[t], xw_two, xs_two)
+            if t > 0:
                 nc.vector.tensor_copy(d_rows[t][:, 0:S], bank[:])
             else:
                 nc.scalar.copy(d_rows[t][:, 0:S], bank[:])
 
-        ds_picked = pick("ds_picked", ds_tab, k1_l, H, U8)
-        for r in range(4):
-            nc.sync.dma_start(ds_plane[r:P:32, :].bitcast(I32), ds_picked[8 * r : P : 32, :].bitcast(I32))
-        nc.vector.tensor_copy(*deal_views(w1_raw, 0, w1_grouped, 0, P))
-        xw_offs = pick("xw_offs", xw_tab, offs_l, S, U32, tag="w1_raw")
-        w1_codes, w1_scales = quantize_weight("w1", w1_grouped, (0, 4))
+        xw_offs = pick("xw_offs", xw_tab, offs_l, S, U32, tag="w2_grouped")
+        dw_picked = pick("dw_picked", dw_tab, k1_l, H, U32)
+        nc.vector.tensor_copy(*deal_views(w1_raw, 0, w1_grouped, W1_SCALAR_M, P))
+        w1_tiles = quantize_weight("w1", w1_grouped, (0, 4))
         y_banks = [psum.tile([P, 2, S], F32, name="y_bank%d" % b) for b in range(2)]
         for t in range(PACK):
-            project(y_banks[t // 2][:, t % 2, :], w1_codes, w1_scales, t, xw_offs, xs_offs)
-        dw_picked = pick("dw_picked", dw_tab, k1_l, H, U32)
+            project(y_banks[t // 2][:, t % 2, :], w1_tiles[t], xw_offs, xs_offs)
 
         h_rows = [sb("h%d" % m, [P, S], F32) for m in range(4)]
         z_planes = sb("z_planes", [P, PACK, S], F32)
 
-        diffs = sb("diffs", [P, PACK, S], F32, tag="dw_tab")
+        diffs = sb("diffs", [P, PACK, S], F32, tag="w1_raw")
         for t in range(PACK):
             g1 = sb("g1_%d" % t, [P, S], F32)
             g2 = sb("g2_%d" % t, [P, S], F32)
             nc.scalar.activation(g1[:], d_rows[t][:].indirect(n1_l[:]), ACT.Copy)
             nc.scalar.activation(g2[:], d_rows[t][:].indirect(n2_l[:]), ACT.Copy)
             nc.vector.tensor_tensor(diffs[:, t, :], g1[:], g2[:], ALU.subtract)
-        for t in range(PACK):
-            th = sb("th_%d" % t, [P, S], F32)
-            nc.scalar.activation(th[:], diffs[:, t, :], ACT.Tanh)
-            nc.vector.scalar_tensor_tensor(z_planes[:, t, :], th[:], gs_t[:, t : t + 1], y_banks[t // 2][:, t % 2, :], ALU.mult, ALU.mult)
-
         halves = [slice(c * N, (c + 1) * N) for c in range(2)]
+        th = sb("th", [P, PACK, S], F32)
+        for t in range(PACK):
+            for cols in (halves if t == PACK - 1 else [slice(0, S)]):
+                nc.scalar.activation(th[:, t, cols], diffs[:, t, cols], ACT.Tanh)
+                nc.vector.scalar_tensor_tensor(z_planes[:, t, cols], th[:, t, cols], gs_t[:, t : t + 1], y_banks[t // 2][:, t % 2, cols], ALU.mult, ALU.mult)
+
         z_grouped = [sb("z_grouped%d" % c, [P, N, PACK], BF16) for c in range(2)]
         z_codes = sb("z_codes", [P, S], U32)
         z_scales = sb("z_scales", [P, S], U8)

@@ -17,19 +17,22 @@ ALU = mybir.AluOpType
 
 P = 128
 PACK = 4
-N = S // 2
-W1_SCALAR_M = 48
-W2_SCALAR_M = 42
+QUADRANTS = 4
+ROW_TILES = H // P
+HALF_S = S // 2
 SPARE = 16
+W2_SCALAR_GROUPS = 48
 
 
-def deal_views(raw, raw_m0, grouped, m0, m1):
-    src = raw[:, :, PACK * (m0 - raw_m0) : PACK * (m1 - raw_m0)].rearrange("p j (m t) -> p m j t", t=PACK)
+def deal_views(raw, grouped, m0, m1):
+    src = raw[:, :, PACK * m0 : PACK * m1].rearrange("p j (m t) -> p m j t", t=PACK)
     dst = grouped[:, :, m0:m1, :].rearrange("p t m j -> p m j t")
     return dst, src
 
 
-def tile_picked_twqjointbkdif_none_p_kernel(tc, x_words, x_scales, w1, w2, gs, d_words, d_scales, offs, two, n1, n2, k1, n3, n4, out):
+def tile_picked_twqjointbkdif_none_p_kernel(
+    tc, x_words, x_scales, w1, w2, gs, d_words, d_scales, offs, two, n1, n2, k1, n3, n4, out
+):
     nc = tc.nc
     with ExitStack() as ctx:
         keep = ctx.enter_context(tc.tile_pool(name="keep", bufs=1))
@@ -43,9 +46,9 @@ def tile_picked_twqjointbkdif_none_p_kernel(tc, x_words, x_scales, w1, w2, gs, d
             nc.sync.dma_start(tile[:], ap)
             return tile
 
-        def load_weight(name, w, c0, c1):
-            tile = sb(name, [P, PACK, c1 - c0], F32)
-            nc.sync.dma_start(tile[:], w.rearrange("(p j) c -> p j c", j=PACK)[:, :, c0:c1])
+        def load_weight(name, w):
+            tile = sb(name, [P, PACK, H], F32)
+            nc.sync.dma_start(tile[:], w.rearrange("(p j) c -> p j c", j=PACK))
             return tile
 
         def load_words(name, words, cols):
@@ -63,18 +66,15 @@ def tile_picked_twqjointbkdif_none_p_kernel(tc, x_words, x_scales, w1, w2, gs, d
         xw_tab = load_words("xw_tab", x_words, T)
         two_l = load_list("two_l", two)
         offs_l = load_list("offs_l", offs)
-        for q in range(4):
+        for q in range(QUADRANTS):
             nc.sync.dma_start(xs_tab[32 * q : 32 * q + 4, :].bitcast(I32), x_scales[0, 4 * q : 4 * q + 4, :].bitcast(I32))
-        w2_raw = load_weight("w2_raw", w2, 0, H)
+        w2_raw = load_weight("w2_raw", w2)
         n1_l = load_list("n1_l", n1)
         n2_l = load_list("n2_l", n2)
-        w1_raw = sb("w1_raw", [P, PACK, H], F32)
-        w1_rows = w1.rearrange("(p j) c -> p j c", j=PACK)
-        nc.sync.dma_start(w1_raw[:, :, 0 : H // 2], w1_rows[:, :, 0 : H // 2])
         k1_l = load_list("k1_l", k1)
         nc.sync.dma_start(ds_tab[0:P:8, :].bitcast(I32), d_scales[0].bitcast(I32))
         dw_tab = load_words("dw_tab", d_words, G)
-        nc.sync.dma_start(w1_raw[:, :, H // 2 : H], w1_rows[:, :, H // 2 : H])
+        w1_raw = load_weight("w1_raw", w1)
         gs_t = sb("gs_t", [P, PACK], F32)
         nc.sync.dma_start(gs_t[:], gs.rearrange("(p t) o -> p (t o)", t=PACK))
         n3_l = load_list("n3_l", n3)
@@ -90,25 +90,34 @@ def tile_picked_twqjointbkdif_none_p_kernel(tc, x_words, x_scales, w1, w2, gs, d
             for t0, t1 in zip(cuts, cuts[1:]):
                 codes = sb("%s_codes%d" % (name, t0), [P, (t1 - t0) * P], U32)
                 scales = sb("%s_scales%d" % (name, t0), [P, (t1 - t0) * P], U8)
-                nc.vector.quantize_mx(codes[:].bitcast(FP8X4), scales[:], grouped[:, t0:t1, :, :].rearrange("p t m j -> p (t m j)"))
+                nc.vector.quantize_mx(
+                    codes[:].bitcast(FP8X4), scales[:], grouped[:, t0:t1, :, :].rearrange("p t m j -> p (t m j)")
+                )
                 for t in range(t1 - t0):
                     tiles.append((codes[:, t * P : (t + 1) * P], scales[:, t * P : (t + 1) * P]))
             return tiles
 
-        def project(bank, weight, xw, xs):
-            codes, scales = weight
-            nc.tensor.matmul_mx(bank, lhsT=codes.bitcast(FP8X4), lhsT_scale=scales,
-                                rhs=xw[:].bitcast(FP8X4), rhs_scale=xs[:], start=True, stop=True)
+        def mx_product(bank, lhs_codes, lhs_scales, rhs_codes, rhs_scales):
+            nc.tensor.matmul_mx(
+                bank,
+                lhsT=lhs_codes.bitcast(FP8X4),
+                lhsT_scale=lhs_scales,
+                rhs=rhs_codes.bitcast(FP8X4),
+                rhs_scale=rhs_scales,
+                start=True,
+                stop=True,
+            )
 
         xs_two = pick("xs_two", xs_tab, two_l, S, U8)
         xw_two = pick("xw_two", xw_tab, two_l, S, U32)
         xs_offs = pick("xs_offs", xs_tab, offs_l, S, U8)
+        xw_offs = pick("xw_offs", xw_tab, offs_l, S, U32)
+
         w2_grouped = sb("w2_grouped", [P, PACK, P, PACK], BF16)
         w1_grouped = sb("w1_grouped", [P, PACK, P, PACK], BF16)
-        nc.scalar.copy(*deal_views(w2_raw, 0, w2_grouped, 0, W2_SCALAR_M))
-        nc.vector.tensor_copy(*deal_views(w2_raw, 0, w2_grouped, W2_SCALAR_M, P))
-        nc.scalar.copy(*deal_views(w1_raw, 0, w1_grouped, 0, W1_SCALAR_M))
-        w2_tiles = quantize_weight("w2", w2_grouped, (0, 1, 4))
+        nc.scalar.copy(*deal_views(w2_raw, w2_grouped, 0, W2_SCALAR_GROUPS))
+        nc.vector.tensor_copy(*deal_views(w2_raw, w2_grouped, W2_SCALAR_GROUPS, P))
+        w2_tiles = quantize_weight("w2", w2_grouped, (0, 1, PACK))
 
         ds_picked = pick("ds_picked", ds_tab, k1_l, H, U8, tag="w2_raw")
         for r in range(4):
@@ -118,63 +127,69 @@ def tile_picked_twqjointbkdif_none_p_kernel(tc, x_words, x_scales, w1, w2, gs, d
         for t in range(PACK):
             nc.vector.memset(d_rows[t][:, S : S + SPARE], 0.0)
         for t in range(PACK):
-            bank = psum.tile([P, S], F32, name="d_bank%d" % t, tag="a%d" % t)
-            project(bank[:], w2_tiles[t], xw_two, xs_two)
+            d_bank = psum.tile([P, S], F32, name="d_bank%d" % t, tag="bank%d" % t)
+            mx_product(d_bank[:], *w2_tiles[t], xw_two[:], xs_two[:])
             if t > 0:
-                nc.vector.tensor_copy(d_rows[t][:, 0:S], bank[:])
+                nc.vector.tensor_copy(d_rows[t][:, 0:S], d_bank[:])
             else:
-                nc.scalar.copy(d_rows[t][:, 0:S], bank[:])
+                nc.scalar.copy(d_rows[t][:, 0:S], d_bank[:])
 
-        xw_offs = pick("xw_offs", xw_tab, offs_l, S, U32, tag="w2_grouped")
         dw_picked = pick("dw_picked", dw_tab, k1_l, H, U32)
-        nc.vector.tensor_copy(*deal_views(w1_raw, 0, w1_grouped, W1_SCALAR_M, P))
-        w1_tiles = quantize_weight("w1", w1_grouped, (0, 4))
-        y_banks = [psum.tile([P, 2, S], F32, name="y_bank%d" % b) for b in range(2)]
+        nc.vector.tensor_copy(*deal_views(w1_raw, w1_grouped, 0, P))
+        w1_tiles = quantize_weight("w1", w1_grouped, (0, PACK))
+        y_banks = [psum.tile([P, 2, S], F32, name="y_bank%d" % b) for b in range(PACK // 2)]
         for t in range(PACK):
-            project(y_banks[t // 2][:, t % 2, :], w1_tiles[t], xw_offs, xs_offs)
+            mx_product(y_banks[t // 2][:, t % 2, :], *w1_tiles[t], xw_offs[:], xs_offs[:])
 
-        h_rows = [sb("h%d" % m, [P, S], F32) for m in range(4)]
-        z_planes = sb("z_planes", [P, PACK, S], F32)
+        h_rows = [sb("h%d" % m, [P, S], F32) for m in range(ROW_TILES)]
+        z_rows = sb("z_rows", [P, PACK, S], F32)
 
         diffs = sb("diffs", [P, PACK, S], F32, tag="w1_raw")
         for t in range(PACK):
-            g1 = sb("g1_%d" % t, [P, S], F32)
-            g2 = sb("g2_%d" % t, [P, S], F32)
-            nc.scalar.activation(g1[:], d_rows[t][:].indirect(n1_l[:]), ACT.Copy)
-            nc.scalar.activation(g2[:], d_rows[t][:].indirect(n2_l[:]), ACT.Copy)
-            nc.vector.tensor_tensor(diffs[:, t, :], g1[:], g2[:], ALU.subtract)
-        halves = [slice(c * N, (c + 1) * N) for c in range(2)]
-        th = sb("th", [P, PACK, S], F32)
-        for t in range(PACK):
-            for cols in (halves if t == PACK - 1 else [slice(0, S)]):
-                nc.scalar.activation(th[:, t, cols], diffs[:, t, cols], ACT.Tanh)
-                nc.vector.scalar_tensor_tensor(z_planes[:, t, cols], th[:, t, cols], gs_t[:, t : t + 1], y_banks[t // 2][:, t % 2, cols], ALU.mult, ALU.mult)
+            d_n1 = sb("d_n1_%d" % t, [P, S], F32)
+            d_n2 = sb("d_n2_%d" % t, [P, S], F32)
+            nc.scalar.activation(d_n1[:], d_rows[t][:].indirect(n1_l[:]), ACT.Copy)
+            nc.scalar.activation(d_n2[:], d_rows[t][:].indirect(n2_l[:]), ACT.Copy)
+            nc.vector.tensor_tensor(diffs[:, t, :], d_n1[:], d_n2[:], ALU.subtract)
 
-        z_grouped = [sb("z_grouped%d" % c, [P, N, PACK], BF16) for c in range(2)]
+        halves = [slice(c * HALF_S, (c + 1) * HALF_S) for c in range(2)]
+        gate = sb("gate", [P, PACK, S], F32)
+        for t in range(PACK):
+            for cols in halves if t == PACK - 1 else [slice(0, S)]:
+                nc.scalar.activation(gate[:, t, cols], diffs[:, t, cols], ACT.Tanh)
+                nc.vector.scalar_tensor_tensor(
+                    z_rows[:, t, cols], gate[:, t, cols], gs_t[:, t : t + 1], y_banks[t // 2][:, t % 2, cols], ALU.mult, ALU.mult
+                )
+
+        z_grouped = [sb("z_grouped%d" % c, [P, HALF_S, PACK], BF16) for c in range(2)]
         z_codes = sb("z_codes", [P, S], U32)
         z_scales = sb("z_scales", [P, S], U8)
         for c in range(2):
-            nc.vector.tensor_copy(z_grouped[c][:].rearrange("p (a i) t -> p a t i", i=4), z_planes[:, :, halves[c]].rearrange("p t (a i) -> p a t i", i=4))
+            nc.vector.tensor_copy(
+                z_grouped[c][:].rearrange("p (a i) t -> p a t i", i=4),
+                z_rows[:, :, halves[c]].rearrange("p t (a i) -> p a t i", i=4),
+            )
         for c in range(2):
-            nc.vector.quantize_mx(z_codes[:, halves[c]].bitcast(FP8X4), z_scales[:, halves[c]], z_grouped[c][:].rearrange("p j t -> p (j t)"))
+            nc.vector.quantize_mx(
+                z_codes[:, halves[c]].bitcast(FP8X4), z_scales[:, halves[c]], z_grouped[c][:].rearrange("p j t -> p (j t)")
+            )
 
         def coded_product(bank, m, cols):
             rows = slice(m * P, (m + 1) * P)
-            nc.tensor.matmul_mx(bank[:], lhsT=dw_picked[:, rows].bitcast(FP8X4), lhsT_scale=ds_plane[:, rows],
-                                rhs=z_codes[:, cols].bitcast(FP8X4), rhs_scale=z_scales[:, cols], start=True, stop=True)
+            mx_product(bank[:], dw_picked[:, rows], ds_plane[:, rows], z_codes[:, cols], z_scales[:, cols])
 
-        h_left = psum.tile([P, N], F32, name="h_left")
+        h_left = psum.tile([P, HALF_S], F32, name="h_left")
         coded_product(h_left, 0, halves[0])
         nc.scalar.activation(h_rows[0][:, halves[0]], h_left[:], ACT.Copy, scale=0.0625)
-        h_right = psum.tile([P, N], F32, name="h_right", tag="a0")
+        h_right = psum.tile([P, HALF_S], F32, name="h_right", tag="bank0")
         coded_product(h_right, 0, halves[1])
         nc.vector.tensor_scalar_mul(h_rows[0][:, halves[1]], h_right[:], 0.0625)
-        for m in range(1, 4):
-            h_bank = psum.tile([P, S], F32, name="h_bank%d" % m, tag="a%d" % m)
+        for m in range(1, ROW_TILES):
+            h_bank = psum.tile([P, S], F32, name="h_bank%d" % m, tag="bank%d" % m)
             coded_product(h_bank, m, slice(0, S))
             nc.vector.tensor_scalar_mul(h_rows[m][:], h_bank[:], 0.0625)
 
-        for m in range(4):
+        for m in range(ROW_TILES):
             old = sb("old%d" % m, [P, W], F32)
             pa = sb("pa%d" % m, [P, W], F32)
             nc.scalar.activation(old[:], h_rows[m][:].indirect(n3_l[:]), ACT.Copy)

from contextlib import ExitStack

import concourse.mybir as mybir

K, T, S, H, G, W = 512, 1024, 256, 512, 2048, 192
FLOPS = 3 * 2 * K * H * S

F32 = mybir.dt.float32
BF16 = mybir.dt.bfloat16
I32 = mybir.dt.int32
U32 = mybir.dt.uint32
U16 = mybir.dt.uint16
U8 = mybir.dt.uint8
FP8X4 = mybir.dt.float8_e4m3fn_x4
ACT = mybir.ActivationFunctionType
ALU = mybir.AluOpType

P = 128
PACK = 4
QUADRANTS = 4
ROW_TILES = H // P
HALF_S = S // 2
SPARE = 16
W2_SCALAR_GROUPS = 48


def deal_views(raw, grouped, m0, m1):
    src = raw[:, :, PACK * m0 : PACK * m1].rearrange("p j (m t) -> p m j t", t=PACK)
    dst = grouped[:, :, m0:m1, :].rearrange("p t m j -> p m j t")
    return dst, src


def tile_picked_twqjointbkdif_none_p_kernel(
    tc, x_words, x_scales, w1, w2, gs, d_words, d_scales, offs, two, n1, n2, k1, n3, n4, out
):
    nc = tc.nc
    with ExitStack() as ctx:
        keep = ctx.enter_context(tc.tile_pool(name="keep", bufs=1))
        psum = ctx.enter_context(tc.psum_pool(name="psum", bufs=1))

        def sb(name, shape, dtype, tag=None):
            return keep.tile(shape, dtype, name=name, tag=tag or name, align_bytes=64)

        def load_list(name, ap):
            tile = sb(name, list(ap.shape), U16)
            nc.sync.dma_start(tile[:], ap)
            return tile

        def load_weight(name, w):
            tile = sb(name, [P, PACK, H], F32)
            nc.sync.dma_start(tile[:], w.rearrange("(p j) c -> p j c", j=PACK))
            return tile

        def load_words(name, words, cols):
            tile = sb(name, [P, cols], U32)
            nc.sync.dma_start(tile[:].bitcast(I32), words[0].rearrange("p n t -> p (n t)").bitcast(I32))
            return tile

        xs_tab = sb("xs_tab", [P, T], U8)
        ds_tab = sb("ds_tab", [P, G], U8)
        ds_plane = sb("ds_plane", [P, H], U8)
        nc.vector.memset(xs_tab[:].bitcast(I32), 0)
        nc.vector.memset(ds_tab[:].bitcast(I32), 0)
        nc.vector.memset(ds_plane[:].bitcast(I32), 0)

        xw_tab = load_words("xw_tab", x_words, T)
        two_l = load_list("two_l", two)
        offs_l = load_list("offs_l", offs)
        for q in range(QUADRANTS):
            nc.sync.dma_start(xs_tab[32 * q : 32 * q + 4, :].bitcast(I32), x_scales[0, 4 * q : 4 * q + 4, :].bitcast(I32))
        w2_raw = load_weight("w2_raw", w2)
        n1_l = load_list("n1_l", n1)
        n2_l = load_list("n2_l", n2)
        k1_l = load_list("k1_l", k1)
        nc.sync.dma_start(ds_tab[0:P:8, :].bitcast(I32), d_scales[0].bitcast(I32))
        dw_tab = load_words("dw_tab", d_words, G)
        w1_raw = load_weight("w1_raw", w1)
        gs_t = sb("gs_t", [P, PACK], F32)
        nc.sync.dma_start(gs_t[:], gs.rearrange("(p t) o -> p (t o)", t=PACK))
        n3_l = load_list("n3_l", n3)
        n4_l = load_list("n4_l", n4)

        def pick(name, table, lst, n, dtype, tag=None):
            tile = sb(name, [P, n], dtype, tag)
            nc.vector.tensor_copy(tile[:], table[:].indirect(lst[:]))
            return tile

        def quantize_weight(name, grouped, cuts):
            tiles = []
            for t0, t1 in zip(cuts, cuts[1:]):
                codes = sb("%s_codes%d" % (name, t0), [P, (t1 - t0) * P], U32)
                scales = sb("%s_scales%d" % (name, t0), [P, (t1 - t0) * P], U8)
                nc.vector.quantize_mx(
                    codes[:].bitcast(FP8X4), scales[:], grouped[:, t0:t1, :, :].rearrange("p t m j -> p (t m j)")
                )
                for t in range(t1 - t0):
                    tiles.append((codes[:, t * P : (t + 1) * P], scales[:, t * P : (t + 1) * P]))
            return tiles

        def mx_product(bank, lhs_codes, lhs_scales, rhs_codes, rhs_scales):
            nc.tensor.matmul_mx(
                bank,
                lhsT=lhs_codes.bitcast(FP8X4),
                lhsT_scale=lhs_scales,
                rhs=rhs_codes.bitcast(FP8X4),
                rhs_scale=rhs_scales,
                start=True,
                stop=True,
            )

        xs_two = pick("xs_two", xs_tab, two_l, S, U8)
        xw_two = pick("xw_two", xw_tab, two_l, S, U32)
        xs_offs = pick("xs_offs", xs_tab, offs_l, S, U8)
        xw_offs = pick("xw_offs", xw_tab, offs_l, S, U32)

        w2_grouped = sb("w2_grouped", [P, PACK, P, PACK], BF16)
        w1_grouped = sb("w1_grouped", [P, PACK, P, PACK], BF16)
        nc.scalar.copy(*deal_views(w2_raw, w2_grouped, 0, W2_SCALAR_GROUPS))
        nc.vector.tensor_copy(*deal_views(w2_raw, w2_grouped, W2_SCALAR_GROUPS, P))
        w2_tiles = quantize_weight("w2", w2_grouped, (0, 1, PACK))

        ds_picked = pick("ds_picked", ds_tab, k1_l, H, U8, tag="w2_raw")
        for r in range(4):
            nc.sync.dma_start(ds_plane[r:P:32, :].bitcast(I32), ds_picked[8 * r : P : 32, :].bitcast(I32))

        d_rows = [sb("d%d" % t, [P, S + SPARE], F32) for t in range(PACK)]
        for t in range(PACK):
            nc.vector.memset(d_rows[t][:, S : S + SPARE], 0.0)
        for t in range(PACK):
            d_bank = psum.tile([P, S], F32, name="d_bank%d" % t, tag="bank%d" % t)
            mx_product(d_bank[:], *w2_tiles[t], xw_two[:], xs_two[:])
            if t > 0:
                nc.vector.tensor_copy(d_rows[t][:, 0:S], d_bank[:])
            else:
                nc.scalar.copy(d_rows[t][:, 0:S], d_bank[:])

        dw_picked = pick("dw_picked", dw_tab, k1_l, H, U32)
        nc.vector.tensor_copy(*deal_views(w1_raw, w1_grouped, 0, P))
        w1_tiles = quantize_weight("w1", w1_grouped, (0, PACK))
        y_banks = [psum.tile([P, 2, S], F32, name="y_bank%d" % b) for b in range(PACK // 2)]
        for t in range(PACK):
            mx_product(y_banks[t // 2][:, t % 2, :], *w1_tiles[t], xw_offs[:], xs_offs[:])

        h_rows = [sb("h%d" % m, [P, S], F32) for m in range(ROW_TILES)]
        z_rows = sb("z_rows", [P, PACK, S], F32)

        diffs = sb("diffs", [P, PACK, S], F32, tag="w1_raw")
        for t in range(PACK):
            d_n1 = sb("d_n1_%d" % t, [P, S], F32)
            d_n2 = sb("d_n2_%d" % t, [P, S], F32)
            nc.scalar.activation(d_n1[:], d_rows[t][:].indirect(n1_l[:]), ACT.Copy)
            nc.scalar.activation(d_n2[:], d_rows[t][:].indirect(n2_l[:]), ACT.Copy)
            nc.vector.tensor_tensor(diffs[:, t, :], d_n1[:], d_n2[:], ALU.subtract)

        halves = [slice(c * HALF_S, (c + 1) * HALF_S) for c in range(2)]
        gate = sb("gate", [P, PACK, S], F32)
        for t in range(PACK):
            for cols in halves if t == PACK - 1 else [slice(0, S)]:
                nc.scalar.activation(gate[:, t, cols], diffs[:, t, cols], ACT.Tanh)
                nc.vector.scalar_tensor_tensor(
                    z_rows[:, t, cols], gate[:, t, cols], gs_t[:, t : t + 1], y_banks[t // 2][:, t % 2, cols], ALU.mult, ALU.mult
                )

        z_grouped = [sb("z_grouped%d" % c, [P, HALF_S, PACK], BF16) for c in range(2)]
        z_codes = sb("z_codes", [P, S], U32)
        z_scales = sb("z_scales", [P, S], U8)
        for c in range(2):
            nc.vector.tensor_copy(
                z_grouped[c][:].rearrange("p (a i) t -> p a t i", i=4),
                z_rows[:, :, halves[c]].rearrange("p t (a i) -> p a t i", i=4),
            )
        for c in range(2):
            nc.vector.quantize_mx(
                z_codes[:, halves[c]].bitcast(FP8X4), z_scales[:, halves[c]], z_grouped[c][:].rearrange("p j t -> p (j t)")
            )

        def coded_product(bank, m, cols):
            rows = slice(m * P, (m + 1) * P)
            mx_product(bank[:], dw_picked[:, rows], ds_plane[:, rows], z_codes[:, cols], z_scales[:, cols])

        h_left = psum.tile([P, HALF_S], F32, name="h_left")
        coded_product(h_left, 0, halves[0])
        nc.scalar.activation(h_rows[0][:, halves[0]], h_left[:], ACT.Copy, scale=0.0625)
        h_right = psum.tile([P, HALF_S], F32, name="h_right", tag="bank0")
        coded_product(h_right, 0, halves[1])
        nc.vector.tensor_scalar_mul(h_rows[0][:, halves[1]], h_right[:], 0.0625)
        for m in range(1, ROW_TILES):
            h_bank = psum.tile([P, S], F32, name="h_bank%d" % m, tag="bank%d" % m)
            coded_product(h_bank, m, slice(0, S))
            nc.vector.tensor_scalar_mul(h_rows[m][:], h_bank[:], 0.0625)

        for m in range(ROW_TILES):
            old = sb("old%d" % m, [P, W], F32)
            pa = sb("pa%d" % m, [P, W], F32)
            nc.scalar.activation(old[:], h_rows[m][:].indirect(n3_l[:]), ACT.Copy)
            nc.scalar.activation(pa[:], h_rows[m][:].indirect(n4_l[:]), ACT.Copy)
            ra = sb("ra%d" % m, [P, W], F32)
            nc.vector.scalar_tensor_tensor(ra[:], pa[:], -0.5, old[:], ALU.mult, ALU.add)
            nc.scalar.activation(h_rows[m][:].indirect(n3_l[:]), ra[:], ACT.Copy)
            nc.sync.dma_start(out[m * P : (m + 1) * P, :], h_rows[m][:])
